import numpy as np
import ml_dtypes


def mxq(x, axis, fmt="e4m3"):
    dtype, down = {"e4m3": (ml_dtypes.float8_e4m3fn, 7), "e5m2": (ml_dtypes.float8_e5m2, 14)}[fmt]
    v = np.moveaxis(np.asarray(x, np.float32).astype(ml_dtypes.bfloat16).astype(np.float64), axis, -1)
    blocks = v.reshape(v.shape[:-1] + (-1, 32))
    amax = np.abs(blocks).max(-1, keepdims=True)
    byte = np.maximum(np.where(amax > 0, np.frexp(amax)[1] - 1 + 127, 0) - down, 1)
    scale = np.exp2(byte - 127.0)
    codes = (blocks / scale).astype(np.float32).astype(dtype).astype(np.float64)
    return np.moveaxis((codes * scale).reshape(v.shape), -1, axis)


WIDE = False


def mx_kscale(k):
    if not WIDE:
        return np.ones(k)
    levels = np.array([30, -30])
    if k % 512:
        return np.exp2(np.random.permutation(np.resize(levels, k // 32))).repeat(32)
    a = np.empty((k // 512, 16))
    for p in range(k // 512):
        a[p, :8] = np.random.permutation(np.resize(levels, 8))
        for g in range(8):
            far = levels[np.abs(levels - a[p, g]) >= 10]
            a[p, g + 8] = far[np.random.randint(len(far))]
    return np.exp2(a.ravel()).repeat(32)


def f64(x):
    return np.asarray(x).astype(np.float64)


def striped(idx):
    return np.tile(np.asarray(idx).reshape(-1, 16).T, (8, 1)).astype(np.uint16)


def unstriped(offs):
    return offs[:16].T.reshape(-1).astype(np.int64)


E2M1 = np.array([0.0, 0.5, 1.0, 1.5, 2.0, 3.0, 4.0, 6.0, -0.0, -0.5, -1.0, -1.5, -2.0, -3.0, -4.0, -6.0])


def pack_weight(w, fmt):
    k, n = w.shape
    w = f64(np.asarray(w, np.float32).astype(ml_dtypes.bfloat16)).reshape(k // 32, 32, n)
    amax = np.abs(w).max(1)
    if fmt in ("e4m3", "e5m2"):
        byte = np.frexp(amax)[1] - 1 + 127 - (7 if fmt == "e4m3" else 14)
    else:
        mant, ex = np.frexp(amax / 6.0)
        byte = np.where(mant > 0.5, ex, ex - 1) + 127
    byte = np.clip(np.where(amax > 0, byte, 1), 1, 254)
    scaled = (w * np.exp2(127.0 - byte)[:, None, :]).reshape(k, n).astype(np.float32)
    by_word = np.ascontiguousarray(scaled.reshape(k // 512, 128, 4, n).transpose(0, 1, 3, 2))
    if fmt in ("e4m3", "e5m2"):
        words = by_word.astype(ml_dtypes.float8_e4m3fn if fmt == "e4m3" else ml_dtypes.float8_e5m2).view(np.uint8)
    else:
        c = by_word.astype(ml_dtypes.float4_e2m1fn).view(np.uint8) & 0xF
        words = (c[..., 0::2] | (c[..., 1::2] << 4)).reshape(k // 512, 128, 2 * n)
    return np.ascontiguousarray(words), np.ascontiguousarray(byte.astype(np.uint8).reshape(k // 512, 16, n))


def unpack_weight(words, scales, fmt):
    g, _, n = scales.shape
    words = np.ascontiguousarray(words).reshape(g, 128, n, -1)
    if fmt in ("e4m3", "e5m2"):
        vals = words.view(ml_dtypes.float8_e4m3fn if fmt == "e4m3" else ml_dtypes.float8_e5m2).astype(np.float64)
    else:
        nib = np.empty((g, 128, n, 4), np.uint8)
        nib[..., 0::2] = words & 0xF
        nib[..., 1::2] = words >> 4
        vals = E2M1[nib]
    vals = vals * np.repeat(np.exp2(scales.astype(np.float64) - 127.0), 8, axis=1)[..., None]
    return vals.transpose(0, 1, 3, 2).reshape(g * 512, n)


def e4m3fn_bytes(y):
    return np.clip(np.asarray(y, np.float64), -448.0, 448.0).astype(np.float32).astype(ml_dtypes.float8_e4m3fn).view(np.uint8)


def e4m3fn_values(b):
    return np.asarray(b, np.uint8).view(ml_dtypes.float8_e4m3fn).astype(np.float64)


K, T, J, R, C, V, O, N = 512, 1024, 256, 512, 512, 1024, 256, 256


def setup_inputs():
    n = np.random.standard_normal
    idx = np.random.permutation(T)[:J]
    idx2 = np.random.permutation(C)[:J]
    idx3 = np.random.permutation(C)[:O]
    idx4 = np.random.permutation(V)[:O]
    fk = mx_kscale(K)
    fr = mx_kscale(R)
    xtp = pack_weight(n((K, T)) / fk[:, None], "e2m1")
    wp = pack_weight(n((K, R)) * 1 / np.sqrt(K) * fk[:, None] * fr, "e5m2")
    wbp = pack_weight(n((R, N)) * 1 / np.sqrt(R) / fr[:, None], "e4m3")
    return {
        "xt_words": xtp[0],
        "xt_scales": xtp[1],
        "w_words": wp[0],
        "w_scales": wp[1],
        "ca": e4m3fn_bytes(60.0 * n((R, V))),
        "st": (np.random.uniform(0.008, 0.024, (R, 1)) * fr[:, None]).astype(np.float32),
        "wb_words": wbp[0],
        "wb_scales": wbp[1],
        "offs": striped(idx),
        "offs2": striped(idx2),
        "offs3": striped(idx3),
        "offs4": striped(idx4),
    }


def reference(xt_words, xt_scales, w_words, w_scales, ca, st, wb_words, wb_scales, offs, offs2, offs3, offs4):
    idx = unstriped(offs)
    idx2 = unstriped(offs2)
    idx3 = unstriped(offs3)
    idx4 = unstriped(offs4)
    xtu = unpack_weight(xt_words, xt_scales, "e2m1")
    wu = unpack_weight(w_words, w_scales, "e5m2")
    wbu = unpack_weight(wb_words, wb_scales, "e4m3")
    xtidxg = xtu[:, idx]
    a = wu.T @ xtidxg
    pw = np.zeros((R, C))
    pw[:, idx2] = a
    g1 = e4m3fn_values(ca)[:, idx4] * f64(st)
    hid = np.maximum(pw[:, idx3] + g1, 0.0)
    hidq = mxq(hid, 0, "e4m3")
    p = wbu.T @ hidq
    return p

@@ -1,0 +1,158 @@
+from contextlib import ExitStack
+
+import concourse.mybir as mybir
+
+K, T, J, R, C, V, O, N = 512, 1024, 256, 512, 512, 1024, 256, 256
+FLOPS = 2 * K * R * J + 2 * R * N * O
+
+F32 = mybir.dt.float32
+BF16 = mybir.dt.bfloat16
+I32 = mybir.dt.int32
+U32 = mybir.dt.uint32
+U16 = mybir.dt.uint16
+U8 = mybir.dt.uint8
+FP8 = mybir.dt.float8_e4m3fn
+E4M3X4 = mybir.dt.float8_e4m3fn_x4
+E5M2X4 = mybir.dt.float8_e5m2_x4
+E2M1X4 = mybir.dt.float4_e2m1fn_x4
+ACT = mybir.ActivationFunctionType
+ALU = mybir.AluOpType
+
+P = 128
+PACK = 4
+QUADS = 4
+HALF = O // 2
+
+
+def tile_list_boardoffset_kernel(tc, xt_words, xt_scales, w_words, w_scales, ca, st, wb_words, wb_scales, offs, offs2, offs3, offs4, out):
+    nc = tc.nc
+    with ExitStack() as ctx:
+        sb = ctx.enter_context(tc.tile_pool(name="sb", bufs=1))
+        ps = ctx.enter_context(tc.psum_pool(name="ps", bufs=1))
+
+        token_list = sb.tile([P, J // 16], U16, name="token_list")
+        put_list = sb.tile([P, J // 16], U16, name="put_list")
+        read_list = sb.tile([P, O // 16], U16, name="read_list")
+        shift_list = sb.tile([P, O // 16], U16, name="shift_list")
+        x_words = sb.tile([P, T], U16, name="x_words", align_bytes=64)
+        x_scales = sb.tile([P, T], U8, name="x_scales", align_bytes=64)
+        w_raw = sb.tile([P, R], U32, name="w_raw", align_bytes=64)
+        w_scales_raw = sb.tile([P, QUADS, R], U8, name="w_scales_raw", align_bytes=64)
+        wb_codes = sb.tile([P, N], U32, name="wb_codes", align_bytes=64)
+        wb_plane = sb.tile([P, N], U8, name="wb_plane", align_bytes=64)
+        steps = sb.tile([P, PACK], F32, name="steps")
+        store = [sb.tile([P, V], U8, name="store%d" % t) for t in range(PACK)]
+        board = [sb.tile([P, C], F32, name="board%d" % t) for t in range(PACK)]
+
+        nc.vector.memset(x_scales[:].bitcast(I32), 0)
+        nc.vector.memset(w_scales_raw[:, 0, :].bitcast(I32), 0)
+        nc.vector.memset(wb_plane[:].bitcast(I32), 0)
+        for t in range(PACK):
+            nc.vector.memset(board[t][:], 0.0)
+
+        ca_rows = ca.rearrange("(p t) v -> t p v", t=PACK)
+        nc.sync.dma_start(x_words[:].bitcast(I32), xt_words[0].bitcast(I32))
+        nc.sync.dma_start(token_list[:], offs)
+        nc.sync.dma_start(w_raw[:].bitcast(I32), w_words[0].rearrange("p c t -> p (c t)").bitcast(I32))
+        nc.sync.dma_start(
+            w_scales_raw[0:4, :, :].bitcast(I32),
+            w_scales[0].rearrange("(q r) c -> r q c", r=4).bitcast(I32),
+        )
+        for q in range(QUADS):
+            nc.sync.dma_start(x_scales[32 * q : 32 * q + 4, :].bitcast(I32), xt_scales[0, 4 * q : 4 * q + 4, :].bitcast(I32))
+        nc.sync.dma_start(shift_list[:], offs4)
+        nc.sync.dma_start(store[0][:], ca_rows[0])
+        nc.sync.dma_start(put_list[:], offs2)
+        nc.sync.dma_start(steps[:], st.rearrange("(p t) o -> p (t o)", t=PACK))
+        for t in range(1, PACK):
+            nc.sync.dma_start(store[t][:], ca_rows[t])
+        nc.sync.dma_start(read_list[:], offs3)
+        nc.sync.dma_start(wb_codes[:].bitcast(I32), wb_words[0].rearrange("p c t -> p (c t)").bitcast(I32))
+        for q in range(QUADS):
+            nc.sync.dma_start(wb_plane[32 * q : 32 * q + 4, :].bitcast(I32), wb_scales[0, 4 * q : 4 * q + 4, :].bitcast(I32))
+
+        w_codes = sb.tile([P, R], U32, name="w_codes", align_bytes=64)
+        w_plane = sb.tile([P, R], U8, name="w_plane", align_bytes=64)
+        nc.scalar.copy(
+            w_codes[:].rearrange("p (t c i) -> p c t i", t=PACK, i=4),
+            w_raw[:].rearrange("p (c i t) -> p c t i", t=PACK, i=4),
+        )
+        for q in range(1, QUADS):
+            nc.vector.tensor_copy(w_scales_raw[32 * q : 32 * q + 4, 0, :].bitcast(I32), w_scales_raw[0:4, q, :].bitcast(I32))
+        nc.vector.tensor_copy(
+            w_plane[:].rearrange("p (t m) -> p t m", t=PACK),
+            w_scales_raw[:, 0, :].rearrange("p (m t) -> p t m", t=PACK),
+        )
+
+        picked_words = sb.tile([P, J], U16, name="picked_words", align_bytes=64)
+        picked_plane = sb.tile([P, J], U8, name="picked_plane", align_bytes=64)
+        nc.vector.tensor_copy(picked_words[:], x_words[:].indirect(token_list[:]))
+        nc.vector.tensor_copy(picked_plane[:], x_scales[:].indirect(token_list[:]))
+
+        hidden = [sb.tile([P, J], F32, name="hidden%d" % t) for t in range(PACK)]
+        banks = [ps.tile([P, J], F32, name="first%d" % t) for t in range(PACK)]
+        order = (0, 3, 1, 2)
+        for t in order:
+            cols = slice(t * P, (t + 1) * P)
+            nc.tensor.matmul_mx(
+                out=banks[t][:],
+                lhsT=w_codes[:, cols].bitcast(E5M2X4),
+                lhsT_scale=w_plane[:, cols],
+                rhs=picked_words[:].bitcast(E2M1X4),
+                rhs_scale=picked_plane[:],
+                start=True,
+                stop=True,
+            )
+        for t in (0, 3):
+            nc.scalar.activation(hidden[t][:], banks[t][:], ACT.Copy)
+        nc.scalar.activation(board[0][:].indirect(put_list[:]), hidden[0][:], ACT.Copy)
+        for t in (1, 2):
+            nc.scalar.activation(hidden[t][:], banks[t][:], ACT.Copy)
+            nc.scalar.activation(board[t][:].indirect(put_list[:]), hidden[t][:], ACT.Copy)
+
+        codes = sb.tile([P, PACK, O], U8, name="codes")
+        shifts = sb.tile([P, PACK, O], F32, name="shifts")
+        for t in range(PACK):
+            nc.vector.tensor_copy(codes[:, t, :], store[t][:].indirect(shift_list[:]))
+        for t in range(PACK):
+            nc.vector.tensor_scalar(shifts[:, t, :], codes[:, t, :].bitcast(FP8), steps[:, t : t + 1], None, ALU.mult)
+        nc.vector.tensor_copy(board[3][:].indirect(put_list[:]), hidden[3][:])
+
+        sums = sb.tile([P, PACK, O], F32, name="sums")
+        for t in (0, 3, 1):
+            nc.vector.tensor_tensor(sums[:, t, :], board[t][:].indirect(read_list[:]), shifts[:, t, :], ALU.add)
+        halves = [slice(h * HALF, (h + 1) * HALF) for h in range(2)]
+        for h in range(2):
+            nc.vector.tensor_tensor(
+                sums[:, 2, halves[h]],
+                board[2][:].indirect(read_list[:, h * HALF // 16 : (h + 1) * HALF // 16]),
+                shifts[:, 2, halves[h]],
+                ALU.add,
+            )
+        woven = [sb.tile([P, HALF, PACK], BF16, name="woven%d" % h, align_bytes=64) for h in range(2)]
+        nc.scalar.activation(woven[0][:], sums[:, :, halves[0]].rearrange("p t o -> p o t"), ACT.Relu)
+        nc.vector.tensor_scalar(woven[1][:], sums[:, :, halves[1]].rearrange("p t o -> p o t"), 0.0, None, ALU.max)
+
+        out_rows = out.rearrange("(a p) o -> p a o", p=P)
+        for h in range(2):
+            hid_codes = sb.tile([P, HALF], U32, name="hid_codes%d" % h, align_bytes=64)
+            hid_plane = sb.tile([P, HALF], U8, name="hid_plane%d" % h, align_bytes=64)
+            nc.vector.quantize_mx(hid_codes[:].bitcast(E4M3X4), hid_plane[:], woven[h][:].rearrange("p o t -> p (o t)"))
+            acc = ps.tile([P, 2, HALF], F32, name="second%d" % h)
+            for a in range(2):
+                cols = slice(a * P, (a + 1) * P)
+                nc.tensor.matmul_mx(
+                    out=acc[:, a, :],
+                    lhsT=wb_codes[:, cols].bitcast(E4M3X4),
+                    lhsT_scale=wb_plane[:, cols],
+                    rhs=hid_codes[:].bitcast(E4M3X4),
+                    rhs_scale=hid_plane[:],
+                    start=True,
+                    stop=True,
+                )
+            result = sb.tile([P, 2, HALF], F32, name="result%d" % h)
+            if h == 0:
+                nc.scalar.activation(result[:], acc[:], ACT.Copy)
+            else:
+                nc.vector.tensor_copy(result[:], acc[:])
+            nc.sync.dma_start(out_rows[:, :, halves[h]], result[:])

@@ -22,6 +22,7 @@ P = 128
 PACK = 4
 QUADS = 4
 HALF = O // 2
+SCALAR_PUTS = 128
 
 
 def tile_list_boardoffset_kernel(tc, xt_words, xt_scales, w_words, w_scales, ca, st, wb_words, wb_scales, offs, offs2, offs3, offs4, out):
@@ -37,29 +38,29 @@ def tile_list_boardoffset_kernel(tc, xt_words, xt_scales, w_words, w_scales, ca,
         x_words = sb.tile([P, T], U16, name="x_words", align_bytes=64)
         x_scales = sb.tile([P, T], U8, name="x_scales", align_bytes=64)
         w_raw = sb.tile([P, R], U32, name="w_raw", align_bytes=64)
-        w_scales_raw = sb.tile([P, QUADS, R], U8, name="w_scales_raw", align_bytes=64)
+        w_rows = sb.tile([4, QUADS, R], U8, name="w_rows", align_bytes=64)
+        w_plane_raw = sb.tile([P, R], U8, name="w_plane_raw", align_bytes=64)
         wb_codes = sb.tile([P, N], U32, name="wb_codes", align_bytes=64)
         wb_plane = sb.tile([P, N], U8, name="wb_plane", align_bytes=64)
-        steps = sb.tile([P, PACK], F32, name="steps")
+        steps = sb.tile([P, PACK], F32, name="steps", tag="steps_then_sums")
         store = [sb.tile([P, V], U8, name="store%d" % t) for t in range(PACK)]
         board = [sb.tile([P, C], F32, name="board%d" % t) for t in range(PACK)]
 
-        nc.vector.memset(x_scales[:].bitcast(I32), 0)
-        nc.vector.memset(w_scales_raw[:, 0, :].bitcast(I32), 0)
+        nc.vector.memset(w_plane_raw[:].bitcast(I32), 0)
         nc.vector.memset(wb_plane[:].bitcast(I32), 0)
         for t in range(PACK):
             nc.vector.memset(board[t][:], 0.0)
 
         ca_rows = ca.rearrange("(p t) v -> t p v", t=PACK)
-        nc.sync.dma_start(x_words[:].bitcast(I32), xt_words[0].bitcast(I32))
-        nc.sync.dma_start(token_list[:], offs)
-        nc.sync.dma_start(w_raw[:].bitcast(I32), w_words[0].rearrange("p c t -> p (c t)").bitcast(I32))
-        nc.sync.dma_start(
-            w_scales_raw[0:4, :, :].bitcast(I32),
-            w_scales[0].rearrange("(q r) c -> r q c", r=4).bitcast(I32),
-        )
+        nc.sync.dma_start(w_rows[:].bitcast(I32), w_scales[0].rearrange("(q r) c -> r q c", r=4).bitcast(I32))
         for q in range(QUADS):
-            nc.sync.dma_start(x_scales[32 * q : 32 * q + 4, :].bitcast(I32), xt_scales[0, 4 * q : 4 * q + 4, :].bitcast(I32))
+            nc.sync.dma_start(
+                x_scales[32 * q : 32 * q + 32, :].bitcast(I32),
+                xt_scales[0, 4 * q : 4 * q + 4, :].bitcast(I32).partition_broadcast(8),
+            )
+        nc.sync.dma_start(token_list[:], offs)
+        nc.sync.dma_start(x_words[:].bitcast(I32), xt_words[0].bitcast(I32))
+        nc.sync.dma_start(w_raw[:].bitcast(I32), w_words[0].rearrange("p c t -> p (c t)").bitcast(I32))
         nc.sync.dma_start(shift_list[:], offs4)
         nc.sync.dma_start(store[0][:], ca_rows[0])
         nc.sync.dma_start(put_list[:], offs2)
@@ -77,17 +78,17 @@ def tile_list_boardoffset_kernel(tc, xt_words, xt_scales, w_words, w_scales, ca,
             w_codes[:].rearrange("p (t c i) -> p c t i", t=PACK, i=4),
             w_raw[:].rearrange("p (c i t) -> p c t i", t=PACK, i=4),
         )
-        for q in range(1, QUADS):
-            nc.vector.tensor_copy(w_scales_raw[32 * q : 32 * q + 4, 0, :].bitcast(I32), w_scales_raw[0:4, q, :].bitcast(I32))
+        for q in range(QUADS):
+            nc.vector.tensor_copy(w_plane_raw[32 * q : 32 * q + 4, :].bitcast(I32), w_rows[:, q, :].bitcast(I32))
         nc.vector.tensor_copy(
             w_plane[:].rearrange("p (t m) -> p t m", t=PACK),
-            w_scales_raw[:, 0, :].rearrange("p (m t) -> p t m", t=PACK),
+            w_plane_raw[:].rearrange("p (m t) -> p t m", t=PACK),
         )
 
         picked_words = sb.tile([P, J], U16, name="picked_words", align_bytes=64)
         picked_plane = sb.tile([P, J], U8, name="picked_plane", align_bytes=64)
-        nc.vector.tensor_copy(picked_words[:], x_words[:].indirect(token_list[:]))
         nc.vector.tensor_copy(picked_plane[:], x_scales[:].indirect(token_list[:]))
+        nc.vector.tensor_copy(picked_words[:], x_words[:].indirect(token_list[:]))
 
         hidden = [sb.tile([P, J], F32, name="hidden%d" % t) for t in range(PACK)]
         banks = [ps.tile([P, J], F32, name="first%d" % t) for t in range(PACK)]
@@ -103,11 +104,11 @@ def tile_list_boardoffset_kernel(tc, xt_words, xt_scales, w_words, w_scales, ca,
                 start=True,
                 stop=True,
             )
-        for t in (0, 3):
-            nc.scalar.activation(hidden[t][:], banks[t][:], ACT.Copy)
-        nc.scalar.activation(board[0][:].indirect(put_list[:]), hidden[0][:], ACT.Copy)
-        for t in (1, 2):
-            nc.scalar.activation(hidden[t][:], banks[t][:], ACT.Copy)
+        nc.scalar.activation(hidden[0][:], banks[0][:], ACT.Copy)
+        nc.scalar.activation(hidden[3][:], banks[3][:], ACT.Copy)
+        for t in range(3):
+            if t > 0:
+                nc.scalar.activation(hidden[t][:], banks[t][:], ACT.Copy)
             nc.scalar.activation(board[t][:].indirect(put_list[:]), hidden[t][:], ACT.Copy)
 
         codes = sb.tile([P, PACK, O], U8, name="codes")
@@ -116,17 +117,18 @@ def tile_list_boardoffset_kernel(tc, xt_words, xt_scales, w_words, w_scales, ca,
             nc.vector.tensor_copy(codes[:, t, :], store[t][:].indirect(shift_list[:]))
         for t in range(PACK):
             nc.vector.tensor_scalar(shifts[:, t, :], codes[:, t, :].bitcast(FP8), steps[:, t : t + 1], None, ALU.mult)
-        nc.vector.tensor_copy(board[3][:].indirect(put_list[:]), hidden[3][:])
+        nc.vector.tensor_copy(board[3][:].indirect(put_list[:, SCALAR_PUTS // 16 :]), hidden[3][:, SCALAR_PUTS:])
+        nc.scalar.activation(board[3][:].indirect(put_list[:, : SCALAR_PUTS // 16]), hidden[3][:, :SCALAR_PUTS], ACT.Copy)
 
-        sums = sb.tile([P, PACK, O], F32, name="sums")
-        for t in (0, 3, 1):
+        sums = sb.tile([P, PACK, O], F32, name="sums", tag="steps_then_sums")
+        for t in range(3):
             nc.vector.tensor_tensor(sums[:, t, :], board[t][:].indirect(read_list[:]), shifts[:, t, :], ALU.add)
         halves = [slice(h * HALF, (h + 1) * HALF) for h in range(2)]
         for h in range(2):
             nc.vector.tensor_tensor(
-                sums[:, 2, halves[h]],
-                board[2][:].indirect(read_list[:, h * HALF // 16 : (h + 1) * HALF // 16]),
-                shifts[:, 2, halves[h]],
+                sums[:, 3, halves[h]],
+                board[3][:].indirect(read_list[:, h * HALF // 16 : (h + 1) * HALF // 16]),
+                shifts[:, 3, halves[h]],
                 ALU.add,
             )
         woven = [sb.tile([P, HALF, PACK], BF16, name="woven%d" % h, align_bytes=64) for h in range(2)]
@@ -138,11 +140,12 @@ def tile_list_boardoffset_kernel(tc, xt_words, xt_scales, w_words, w_scales, ca,
             hid_codes = sb.tile([P, HALF], U32, name="hid_codes%d" % h, align_bytes=64)
             hid_plane = sb.tile([P, HALF], U8, name="hid_plane%d" % h, align_bytes=64)
             nc.vector.quantize_mx(hid_codes[:].bitcast(E4M3X4), hid_plane[:], woven[h][:].rearrange("p o t -> p (o t)"))
-            acc = ps.tile([P, 2, HALF], F32, name="second%d" % h)
+            result = sb.tile([P, 2, HALF], F32, name="result%d" % h)
             for a in range(2):
+                acc = ps.tile([P, HALF], F32, name="second%d%d" % (h, a))
                 cols = slice(a * P, (a + 1) * P)
                 nc.tensor.matmul_mx(
-                    out=acc[:, a, :],
+                    out=acc[:],
                     lhsT=wb_codes[:, cols].bitcast(E4M3X4),
                     lhsT_scale=wb_plane[:, cols],
                     rhs=hid_codes[:].bitcast(E4M3X4),
@@ -150,9 +153,8 @@ def tile_list_boardoffset_kernel(tc, xt_words, xt_scales, w_words, w_scales, ca,
                     start=True,
                     stop=True,
                 )
-            result = sb.tile([P, 2, HALF], F32, name="result%d" % h)
-            if h == 0:
-                nc.scalar.activation(result[:], acc[:], ACT.Copy)
-            else:
-                nc.vector.tensor_copy(result[:], acc[:])
+                if a == 0:
+                    nc.scalar.activation(result[:, a, :], acc[:], ACT.Copy)
+                else:
+                    nc.vector.tensor_copy(result[:, a, :], acc[:])
             nc.sync.dma_start(out_rows[:, :, halves[h]], result[:])

@@ -22,7 +22,8 @@ P = 128
 PACK = 4
 QUADS = 4
 HALF = O // 2
-SCALAR_PUTS = 128
+SHARED = 1
+SCALAR_PUTS = 64
 
 
 def tile_list_boardoffset_kernel(tc, xt_words, xt_scales, w_words, w_scales, ca, st, wb_words, wb_scales, offs, offs2, offs3, offs4, out):
@@ -35,7 +36,7 @@ def tile_list_boardoffset_kernel(tc, xt_words, xt_scales, w_words, w_scales, ca,
         put_list = sb.tile([P, J // 16], U16, name="put_list")
         read_list = sb.tile([P, O // 16], U16, name="read_list")
         shift_list = sb.tile([P, O // 16], U16, name="shift_list")
-        x_words = sb.tile([P, T], U16, name="x_words", align_bytes=64)
+        x_words = sb.tile([P, T], U16, name="x_words", tag="tokens_then_plane", align_bytes=64)
         x_scales = sb.tile([P, T], U8, name="x_scales", align_bytes=64)
         w_raw = sb.tile([P, R], U32, name="w_raw", align_bytes=64)
         w_rows = sb.tile([4, QUADS, R], U8, name="w_rows", align_bytes=64)
@@ -73,43 +74,41 @@ def tile_list_boardoffset_kernel(tc, xt_words, xt_scales, w_words, w_scales, ca,
             nc.sync.dma_start(wb_plane[32 * q : 32 * q + 4, :].bitcast(I32), wb_scales[0, 4 * q : 4 * q + 4, :].bitcast(I32))
 
         w_codes = sb.tile([P, R], U32, name="w_codes", align_bytes=64)
-        w_plane = sb.tile([P, R], U8, name="w_plane", align_bytes=64)
-        nc.scalar.copy(
-            w_codes[:].rearrange("p (t c i) -> p c t i", t=PACK, i=4),
-            w_raw[:].rearrange("p (c i t) -> p c t i", t=PACK, i=4),
-        )
+        dealt_codes = w_codes[:].rearrange("p (t c i) -> p c t i", t=PACK, i=4)
+        raw_codes = w_raw[:].rearrange("p (c i t) -> p c t i", t=PACK, i=4)
+        nc.scalar.copy(dealt_codes[:, :, :2, :], raw_codes[:, :, :2, :])
+        nc.scalar.copy(dealt_codes[:, :, 2:, :], raw_codes[:, :, 2:, :])
         for q in range(QUADS):
             nc.vector.tensor_copy(w_plane_raw[32 * q : 32 * q + 4, :].bitcast(I32), w_rows[:, q, :].bitcast(I32))
-        nc.vector.tensor_copy(
-            w_plane[:].rearrange("p (t m) -> p t m", t=PACK),
-            w_plane_raw[:].rearrange("p (m t) -> p t m", t=PACK),
-        )
+        raw_plane = w_plane_raw[:].rearrange("p (m t) -> p t m", t=PACK)
+        early_planes = sb.tile([P, 2, P], U8, name="early_planes", align_bytes=64)
+        nc.vector.tensor_copy(early_planes[:], raw_plane[:, :2, :])
 
         picked_words = sb.tile([P, J], U16, name="picked_words", align_bytes=64)
         picked_plane = sb.tile([P, J], U8, name="picked_plane", align_bytes=64)
         nc.vector.tensor_copy(picked_plane[:], x_scales[:].indirect(token_list[:]))
         nc.vector.tensor_copy(picked_words[:], x_words[:].indirect(token_list[:]))
+        late_planes = sb.tile([P, 2, P], U8, name="late_planes", tag="tokens_then_plane", align_bytes=64)
+        nc.vector.tensor_copy(late_planes[:], raw_plane[:, 2:, :])
+        w_planes = [early_planes[:, t, :] for t in range(2)] + [late_planes[:, t, :] for t in range(2)]
 
         hidden = [sb.tile([P, J], F32, name="hidden%d" % t) for t in range(PACK)]
         banks = [ps.tile([P, J], F32, name="first%d" % t) for t in range(PACK)]
-        order = (0, 3, 1, 2)
-        for t in order:
-            cols = slice(t * P, (t + 1) * P)
+        whole = [t for t in range(PACK) if t != SHARED]
+        for t in [SHARED] + whole:
             nc.tensor.matmul_mx(
                 out=banks[t][:],
-                lhsT=w_codes[:, cols].bitcast(E5M2X4),
-                lhsT_scale=w_plane[:, cols],
+                lhsT=w_codes[:, t * P : (t + 1) * P].bitcast(E5M2X4),
+                lhsT_scale=w_planes[t],
                 rhs=picked_words[:].bitcast(E2M1X4),
                 rhs_scale=picked_plane[:],
                 start=True,
                 stop=True,
             )
-        nc.scalar.activation(hidden[0][:], banks[0][:], ACT.Copy)
-        nc.scalar.activation(hidden[3][:], banks[3][:], ACT.Copy)
-        for t in range(3):
-            if t > 0:
-                nc.scalar.activation(hidden[t][:], banks[t][:], ACT.Copy)
-            nc.scalar.activation(board[t][:].indirect(put_list[:]), hidden[t][:], ACT.Copy)
+        for t in [SHARED] + whole:
+            puts = SCALAR_PUTS if t == SHARED else J
+            nc.scalar.activation(hidden[t][:], banks[t][:], ACT.Copy)
+            nc.scalar.activation(board[t][:].indirect(put_list[:, : puts // 16]), hidden[t][:, :puts], ACT.Copy)
 
         codes = sb.tile([P, PACK, O], U8, name="codes")
         shifts = sb.tile([P, PACK, O], F32, name="shifts")
@@ -117,23 +116,25 @@ def tile_list_boardoffset_kernel(tc, xt_words, xt_scales, w_words, w_scales, ca,
             nc.vector.tensor_copy(codes[:, t, :], store[t][:].indirect(shift_list[:]))
         for t in range(PACK):
             nc.vector.tensor_scalar(shifts[:, t, :], codes[:, t, :].bitcast(FP8), steps[:, t : t + 1], None, ALU.mult)
-        nc.vector.tensor_copy(board[3][:].indirect(put_list[:, SCALAR_PUTS // 16 :]), hidden[3][:, SCALAR_PUTS:])
-        nc.scalar.activation(board[3][:].indirect(put_list[:, : SCALAR_PUTS // 16]), hidden[3][:, :SCALAR_PUTS], ACT.Copy)
+        nc.vector.tensor_copy(board[SHARED][:].indirect(put_list[:, SCALAR_PUTS // 16 :]), hidden[SHARED][:, SCALAR_PUTS:])
 
         sums = sb.tile([P, PACK, O], F32, name="sums", tag="steps_then_sums")
-        for t in range(3):
+        last = whole[-1]
+        for t in [whole[0], SHARED, whole[1]]:
             nc.vector.tensor_tensor(sums[:, t, :], board[t][:].indirect(read_list[:]), shifts[:, t, :], ALU.add)
         halves = [slice(h * HALF, (h + 1) * HALF) for h in range(2)]
         for h in range(2):
             nc.vector.tensor_tensor(
-                sums[:, 3, halves[h]],
-                board[3][:].indirect(read_list[:, h * HALF // 16 : (h + 1) * HALF // 16]),
-                shifts[:, 3, halves[h]],
+                sums[:, last, halves[h]],
+                board[last][:].indirect(read_list[:, h * HALF // 16 : (h + 1) * HALF // 16]),
+                shifts[:, last, halves[h]],
                 ALU.add,
             )
         woven = [sb.tile([P, HALF, PACK], BF16, name="woven%d" % h, align_bytes=64) for h in range(2)]
         nc.scalar.activation(woven[0][:], sums[:, :, halves[0]].rearrange("p t o -> p o t"), ACT.Relu)
-        nc.vector.tensor_scalar(woven[1][:], sums[:, :, halves[1]].rearrange("p t o -> p o t"), 0.0, None, ALU.max)
+        cut = HALF // 2
+        nc.vector.tensor_scalar(woven[1][:, :cut, :], sums[:, :, HALF : HALF + cut].rearrange("p t o -> p o t"), 0.0, None, ALU.max)
+        nc.scalar.activation(woven[1][:, cut:, :], sums[:, :, HALF + cut :].rearrange("p t o -> p o t"), ACT.Relu)
 
         out_rows = out.rearrange("(a p) o -> p a o", p=P)
         for h in range(2):

@@ -21,9 +21,15 @@ ALU = mybir.AluOpType
 P = 128
 PACK = 4
 QUADS = 4
+QUAD = P // QUADS
+LIVE = 4
+GROUP = 16
+RUN = 4
 HALF = O // 2
+EARLY = 2
 SHARED = 1
 SCALAR_PUTS = 64
+VECTOR_PLACES = HALF // 2
 
 
 def tile_list_boardoffset_kernel(tc, xt_words, xt_scales, w_words, w_scales, ca, st, wb_words, wb_scales, offs, offs2, offs3, offs4, out):
@@ -32,14 +38,14 @@ def tile_list_boardoffset_kernel(tc, xt_words, xt_scales, w_words, w_scales, ca,
         sb = ctx.enter_context(tc.tile_pool(name="sb", bufs=1))
         ps = ctx.enter_context(tc.psum_pool(name="ps", bufs=1))
 
-        token_list = sb.tile([P, J // 16], U16, name="token_list")
-        put_list = sb.tile([P, J // 16], U16, name="put_list")
-        read_list = sb.tile([P, O // 16], U16, name="read_list")
-        shift_list = sb.tile([P, O // 16], U16, name="shift_list")
+        token_list = sb.tile([P, J // GROUP], U16, name="token_list")
+        put_list = sb.tile([P, J // GROUP], U16, name="put_list")
+        read_list = sb.tile([P, O // GROUP], U16, name="read_list")
+        shift_list = sb.tile([P, O // GROUP], U16, name="shift_list")
         x_words = sb.tile([P, T], U16, name="x_words", tag="tokens_then_plane", align_bytes=64)
         x_scales = sb.tile([P, T], U8, name="x_scales", align_bytes=64)
         w_raw = sb.tile([P, R], U32, name="w_raw", align_bytes=64)
-        w_rows = sb.tile([4, QUADS, R], U8, name="w_rows", align_bytes=64)
+        w_rows = sb.tile([LIVE, QUADS, R], U8, name="w_rows", align_bytes=64)
         w_plane_raw = sb.tile([P, R], U8, name="w_plane_raw", align_bytes=64)
         wb_codes = sb.tile([P, N], U32, name="wb_codes", align_bytes=64)
         wb_plane = sb.tile([P, N], U8, name="wb_plane", align_bytes=64)
@@ -53,11 +59,11 @@ def tile_list_boardoffset_kernel(tc, xt_words, xt_scales, w_words, w_scales, ca,
             nc.vector.memset(board[t][:], 0.0)
 
         ca_rows = ca.rearrange("(p t) v -> t p v", t=PACK)
-        nc.sync.dma_start(w_rows[:].bitcast(I32), w_scales[0].rearrange("(q r) c -> r q c", r=4).bitcast(I32))
+        nc.sync.dma_start(w_rows[:].bitcast(I32), w_scales[0].rearrange("(q r) c -> r q c", r=LIVE).bitcast(I32))
         for q in range(QUADS):
             nc.sync.dma_start(
-                x_scales[32 * q : 32 * q + 32, :].bitcast(I32),
-                xt_scales[0, 4 * q : 4 * q + 4, :].bitcast(I32).partition_broadcast(8),
+                x_scales[QUAD * q : QUAD * (q + 1), :].bitcast(I32),
+                xt_scales[0, LIVE * q : LIVE * (q + 1), :].bitcast(I32).partition_broadcast(QUAD // LIVE),
             )
         nc.sync.dma_start(token_list[:], offs)
         nc.sync.dma_start(x_words[:].bitcast(I32), xt_words[0].bitcast(I32))
@@ -71,26 +77,29 @@ def tile_list_boardoffset_kernel(tc, xt_words, xt_scales, w_words, w_scales, ca,
         nc.sync.dma_start(read_list[:], offs3)
         nc.sync.dma_start(wb_codes[:].bitcast(I32), wb_words[0].rearrange("p c t -> p (c t)").bitcast(I32))
         for q in range(QUADS):
-            nc.sync.dma_start(wb_plane[32 * q : 32 * q + 4, :].bitcast(I32), wb_scales[0, 4 * q : 4 * q + 4, :].bitcast(I32))
+            nc.sync.dma_start(
+                wb_plane[QUAD * q : QUAD * q + LIVE, :].bitcast(I32),
+                wb_scales[0, LIVE * q : LIVE * (q + 1), :].bitcast(I32),
+            )
 
         w_codes = sb.tile([P, R], U32, name="w_codes", align_bytes=64)
-        dealt_codes = w_codes[:].rearrange("p (t c i) -> p c t i", t=PACK, i=4)
-        raw_codes = w_raw[:].rearrange("p (c i t) -> p c t i", t=PACK, i=4)
-        nc.scalar.copy(dealt_codes[:, :, :2, :], raw_codes[:, :, :2, :])
-        nc.scalar.copy(dealt_codes[:, :, 2:, :], raw_codes[:, :, 2:, :])
+        dealt_codes = w_codes[:].rearrange("p (t c i) -> p c t i", t=PACK, i=RUN)
+        raw_codes = w_raw[:].rearrange("p (c i t) -> p c t i", t=PACK, i=RUN)
+        nc.scalar.copy(dealt_codes[:, :, :EARLY, :], raw_codes[:, :, :EARLY, :])
+        nc.scalar.copy(dealt_codes[:, :, EARLY:, :], raw_codes[:, :, EARLY:, :])
         for q in range(QUADS):
-            nc.vector.tensor_copy(w_plane_raw[32 * q : 32 * q + 4, :].bitcast(I32), w_rows[:, q, :].bitcast(I32))
+            nc.vector.tensor_copy(w_plane_raw[QUAD * q : QUAD * q + LIVE, :].bitcast(I32), w_rows[:, q, :].bitcast(I32))
         raw_plane = w_plane_raw[:].rearrange("p (m t) -> p t m", t=PACK)
-        early_planes = sb.tile([P, 2, P], U8, name="early_planes", align_bytes=64)
-        nc.vector.tensor_copy(early_planes[:], raw_plane[:, :2, :])
+        early_planes = sb.tile([P, EARLY, P], U8, name="early_planes", align_bytes=64)
+        nc.vector.tensor_copy(early_planes[:], raw_plane[:, :EARLY, :])
 
         picked_words = sb.tile([P, J], U16, name="picked_words", align_bytes=64)
         picked_plane = sb.tile([P, J], U8, name="picked_plane", align_bytes=64)
         nc.vector.tensor_copy(picked_plane[:], x_scales[:].indirect(token_list[:]))
         nc.vector.tensor_copy(picked_words[:], x_words[:].indirect(token_list[:]))
-        late_planes = sb.tile([P, 2, P], U8, name="late_planes", tag="tokens_then_plane", align_bytes=64)
-        nc.vector.tensor_copy(late_planes[:], raw_plane[:, 2:, :])
-        w_planes = [early_planes[:, t, :] for t in range(2)] + [late_planes[:, t, :] for t in range(2)]
+        late_planes = sb.tile([P, PACK - EARLY, P], U8, name="late_planes", tag="tokens_then_plane", align_bytes=64)
+        nc.vector.tensor_copy(late_planes[:], raw_plane[:, EARLY:, :])
+        w_planes = [early_planes[:, t, :] for t in range(EARLY)] + [late_planes[:, t, :] for t in range(PACK - EARLY)]
 
         hidden = [sb.tile([P, J], F32, name="hidden%d" % t) for t in range(PACK)]
         banks = [ps.tile([P, J], F32, name="first%d" % t) for t in range(PACK)]
@@ -108,7 +117,7 @@ def tile_list_boardoffset_kernel(tc, xt_words, xt_scales, w_words, w_scales, ca,
         for t in [SHARED] + whole:
             puts = SCALAR_PUTS if t == SHARED else J
             nc.scalar.activation(hidden[t][:], banks[t][:], ACT.Copy)
-            nc.scalar.activation(board[t][:].indirect(put_list[:, : puts // 16]), hidden[t][:, :puts], ACT.Copy)
+            nc.scalar.activation(board[t][:].indirect(put_list[:, : puts // GROUP]), hidden[t][:, :puts], ACT.Copy)
 
         codes = sb.tile([P, PACK, O], U8, name="codes")
         shifts = sb.tile([P, PACK, O], F32, name="shifts")
@@ -116,7 +125,7 @@ def tile_list_boardoffset_kernel(tc, xt_words, xt_scales, w_words, w_scales, ca,
             nc.vector.tensor_copy(codes[:, t, :], store[t][:].indirect(shift_list[:]))
         for t in range(PACK):
             nc.vector.tensor_scalar(shifts[:, t, :], codes[:, t, :].bitcast(FP8), steps[:, t : t + 1], None, ALU.mult)
-        nc.vector.tensor_copy(board[SHARED][:].indirect(put_list[:, SCALAR_PUTS // 16 :]), hidden[SHARED][:, SCALAR_PUTS:])
+        nc.vector.tensor_copy(board[SHARED][:].indirect(put_list[:, SCALAR_PUTS // GROUP :]), hidden[SHARED][:, SCALAR_PUTS:])
 
         sums = sb.tile([P, PACK, O], F32, name="sums", tag="steps_then_sums")
         last = whole[-1]
@@ -126,23 +135,28 @@ def tile_list_boardoffset_kernel(tc, xt_words, xt_scales, w_words, w_scales, ca,
         for h in range(2):
             nc.vector.tensor_tensor(
                 sums[:, last, halves[h]],
-                board[last][:].indirect(read_list[:, h * HALF // 16 : (h + 1) * HALF // 16]),
+                board[last][:].indirect(read_list[:, h * HALF // GROUP : (h + 1) * HALF // GROUP]),
                 shifts[:, last, halves[h]],
                 ALU.add,
             )
+
         woven = [sb.tile([P, HALF, PACK], BF16, name="woven%d" % h, align_bytes=64) for h in range(2)]
-        nc.scalar.activation(woven[0][:], sums[:, :, halves[0]].rearrange("p t o -> p o t"), ACT.Relu)
-        cut = HALF // 2
-        nc.vector.tensor_scalar(woven[1][:, :cut, :], sums[:, :, HALF : HALF + cut].rearrange("p t o -> p o t"), 0.0, None, ALU.max)
-        nc.scalar.activation(woven[1][:, cut:, :], sums[:, :, HALF + cut :].rearrange("p t o -> p o t"), ACT.Relu)
+        to_woven = "p (c i) t -> p c t i"
+        from_sums = "p t (c i) -> p c t i"
+        cut = HALF + VECTOR_PLACES
+        nc.scalar.activation(woven[0][:].rearrange(to_woven, i=RUN), sums[:, :, halves[0]].rearrange(from_sums, i=RUN), ACT.Relu)
+        nc.vector.tensor_scalar(
+            woven[1][:, :VECTOR_PLACES, :].rearrange(to_woven, i=RUN), sums[:, :, HALF:cut].rearrange(from_sums, i=RUN), 0.0, None, ALU.max
+        )
+        nc.scalar.activation(woven[1][:, VECTOR_PLACES:, :].rearrange(to_woven, i=RUN), sums[:, :, cut:].rearrange(from_sums, i=RUN), ACT.Relu)
 
         out_rows = out.rearrange("(a p) o -> p a o", p=P)
         for h in range(2):
             hid_codes = sb.tile([P, HALF], U32, name="hid_codes%d" % h, align_bytes=64)
             hid_plane = sb.tile([P, HALF], U8, name="hid_plane%d" % h, align_bytes=64)
             nc.vector.quantize_mx(hid_codes[:].bitcast(E4M3X4), hid_plane[:], woven[h][:].rearrange("p o t -> p (o t)"))
-            result = sb.tile([P, 2, HALF], F32, name="result%d" % h)
-            for a in range(2):
+            result = sb.tile([P, N // P, HALF], F32, name="result%d" % h)
+            for a in range(N // P):
                 acc = ps.tile([P, HALF], F32, name="second%d%d" % (h, a))
                 cols = slice(a * P, (a + 1) * P)
                 nc.tensor.matmul_mx(

from contextlib import ExitStack

import concourse.mybir as mybir

K, T, J, R, C, V, O, N = 512, 1024, 256, 512, 512, 1024, 256, 256
FLOPS = 2 * K * R * J + 2 * R * N * O

F32 = mybir.dt.float32
BF16 = mybir.dt.bfloat16
I32 = mybir.dt.int32
U32 = mybir.dt.uint32
U16 = mybir.dt.uint16
U8 = mybir.dt.uint8
FP8 = mybir.dt.float8_e4m3fn
E4M3X4 = mybir.dt.float8_e4m3fn_x4
E5M2X4 = mybir.dt.float8_e5m2_x4
E2M1X4 = mybir.dt.float4_e2m1fn_x4
ACT = mybir.ActivationFunctionType
ALU = mybir.AluOpType

P = 128
PACK = 4
QUADS = 4
QUAD = P // QUADS
LIVE = 4
GROUP = 16
RUN = 4
HALF = O // 2
EARLY = 2
SHARED = 1
SCALAR_PUTS = 64
VECTOR_PLACES = HALF // 2


def tile_list_boardoffset_kernel(tc, xt_words, xt_scales, w_words, w_scales, ca, st, wb_words, wb_scales, offs, offs2, offs3, offs4, out):
    nc = tc.nc
    with ExitStack() as ctx:
        sb = ctx.enter_context(tc.tile_pool(name="sb", bufs=1))
        ps = ctx.enter_context(tc.psum_pool(name="ps", bufs=1))

        token_list = sb.tile([P, J // GROUP], U16, name="token_list")
        put_list = sb.tile([P, J // GROUP], U16, name="put_list")
        read_list = sb.tile([P, O // GROUP], U16, name="read_list")
        shift_list = sb.tile([P, O // GROUP], U16, name="shift_list")
        x_words = sb.tile([P, T], U16, name="x_words", tag="tokens_then_plane", align_bytes=64)
        x_scales = sb.tile([P, T], U8, name="x_scales", align_bytes=64)
        w_raw = sb.tile([P, R], U32, name="w_raw", align_bytes=64)
        w_rows = sb.tile([LIVE, QUADS, R], U8, name="w_rows", align_bytes=64)
        w_plane_raw = sb.tile([P, R], U8, name="w_plane_raw", align_bytes=64)
        wb_codes = sb.tile([P, N], U32, name="wb_codes", align_bytes=64)
        wb_plane = sb.tile([P, N], U8, name="wb_plane", align_bytes=64)
        steps = sb.tile([P, PACK], F32, name="steps", tag="steps_then_sums")
        store = [sb.tile([P, V], U8, name="store%d" % t) for t in range(PACK)]
        board = [sb.tile([P, C], F32, name="board%d" % t) for t in range(PACK)]

        nc.vector.memset(w_plane_raw[:].bitcast(I32), 0)
        nc.vector.memset(wb_plane[:].bitcast(I32), 0)
        for t in range(PACK):
            nc.vector.memset(board[t][:], 0.0)

        ca_rows = ca.rearrange("(p t) v -> t p v", t=PACK)
        nc.sync.dma_start(w_rows[:].bitcast(I32), w_scales[0].rearrange("(q r) c -> r q c", r=LIVE).bitcast(I32))
        for q in range(QUADS):
            nc.sync.dma_start(
                x_scales[QUAD * q : QUAD * (q + 1), :].bitcast(I32),
                xt_scales[0, LIVE * q : LIVE * (q + 1), :].bitcast(I32).partition_broadcast(QUAD // LIVE),
            )
        nc.sync.dma_start(token_list[:], offs)
        nc.sync.dma_start(x_words[:].bitcast(I32), xt_words[0].bitcast(I32))
        nc.sync.dma_start(w_raw[:].bitcast(I32), w_words[0].rearrange("p c t -> p (c t)").bitcast(I32))
        nc.sync.dma_start(shift_list[:], offs4)
        nc.sync.dma_start(store[0][:], ca_rows[0])
        nc.sync.dma_start(put_list[:], offs2)
        nc.sync.dma_start(steps[:], st.rearrange("(p t) o -> p (t o)", t=PACK))
        for t in range(1, PACK):
            nc.sync.dma_start(store[t][:], ca_rows[t])
        nc.sync.dma_start(read_list[:], offs3)
        nc.sync.dma_start(wb_codes[:].bitcast(I32), wb_words[0].rearrange("p c t -> p (c t)").bitcast(I32))
        for q in range(QUADS):
            nc.sync.dma_start(
                wb_plane[QUAD * q : QUAD * q + LIVE, :].bitcast(I32),
                wb_scales[0, LIVE * q : LIVE * (q + 1), :].bitcast(I32),
            )

        w_codes = sb.tile([P, R], U32, name="w_codes", align_bytes=64)
        dealt_codes = w_codes[:].rearrange("p (t c i) -> p c t i", t=PACK, i=RUN)
        raw_codes = w_raw[:].rearrange("p (c i t) -> p c t i", t=PACK, i=RUN)
        nc.scalar.copy(dealt_codes[:, :, :EARLY, :], raw_codes[:, :, :EARLY, :])
        nc.scalar.copy(dealt_codes[:, :, EARLY:, :], raw_codes[:, :, EARLY:, :])
        for q in range(QUADS):
            nc.vector.tensor_copy(w_plane_raw[QUAD * q : QUAD * q + LIVE, :].bitcast(I32), w_rows[:, q, :].bitcast(I32))
        raw_plane = w_plane_raw[:].rearrange("p (m t) -> p t m", t=PACK)
        early_planes = sb.tile([P, EARLY, P], U8, name="early_planes", align_bytes=64)
        nc.vector.tensor_copy(early_planes[:], raw_plane[:, :EARLY, :])

        picked_words = sb.tile([P, J], U16, name="picked_words", align_bytes=64)
        picked_plane = sb.tile([P, J], U8, name="picked_plane", align_bytes=64)
        nc.vector.tensor_copy(picked_plane[:], x_scales[:].indirect(token_list[:]))
        nc.vector.tensor_copy(picked_words[:], x_words[:].indirect(token_list[:]))
        late_planes = sb.tile([P, PACK - EARLY, P], U8, name="late_planes", tag="tokens_then_plane", align_bytes=64)
        nc.vector.tensor_copy(late_planes[:], raw_plane[:, EARLY:, :])
        w_planes = [early_planes[:, t, :] for t in range(EARLY)] + [late_planes[:, t, :] for t in range(PACK - EARLY)]

        hidden = [sb.tile([P, J], F32, name="hidden%d" % t) for t in range(PACK)]
        banks = [ps.tile([P, J], F32, name="first%d" % t) for t in range(PACK)]
        whole = [t for t in range(PACK) if t != SHARED]
        for t in [SHARED] + whole:
            nc.tensor.matmul_mx(
                out=banks[t][:],
                lhsT=w_codes[:, t * P : (t + 1) * P].bitcast(E5M2X4),
                lhsT_scale=w_planes[t],
                rhs=picked_words[:].bitcast(E2M1X4),
                rhs_scale=picked_plane[:],
                start=True,
                stop=True,
            )
        for t in [SHARED] + whole:
            puts = SCALAR_PUTS if t == SHARED else J
            nc.scalar.activation(hidden[t][:], banks[t][:], ACT.Copy)
            nc.scalar.activation(board[t][:].indirect(put_list[:, : puts // GROUP]), hidden[t][:, :puts], ACT.Copy)

        codes = sb.tile([P, PACK, O], U8, name="codes")
        shifts = sb.tile([P, PACK, O], F32, name="shifts")
        for t in range(PACK):
            nc.vector.tensor_copy(codes[:, t, :], store[t][:].indirect(shift_list[:]))
        for t in range(PACK):
            nc.vector.tensor_scalar(shifts[:, t, :], codes[:, t, :].bitcast(FP8), steps[:, t : t + 1], None, ALU.mult)
        nc.vector.tensor_copy(board[SHARED][:].indirect(put_list[:, SCALAR_PUTS // GROUP :]), hidden[SHARED][:, SCALAR_PUTS:])

        sums = sb.tile([P, PACK, O], F32, name="sums", tag="steps_then_sums")
        last = whole[-1]
        for t in [whole[0], SHARED, whole[1]]:
            nc.vector.tensor_tensor(sums[:, t, :], board[t][:].indirect(read_list[:]), shifts[:, t, :], ALU.add)
        halves = [slice(h * HALF, (h + 1) * HALF) for h in range(2)]
        for h in range(2):
            nc.vector.tensor_tensor(
                sums[:, last, halves[h]],
                board[last][:].indirect(read_list[:, h * HALF // GROUP : (h + 1) * HALF // GROUP]),
                shifts[:, last, halves[h]],
                ALU.add,
            )

        woven = [sb.tile([P, HALF, PACK], BF16, name="woven%d" % h, align_bytes=64) for h in range(2)]
        to_woven = "p (c i) t -> p c t i"
        from_sums = "p t (c i) -> p c t i"
        cut = HALF + VECTOR_PLACES
        nc.scalar.activation(woven[0][:].rearrange(to_woven, i=RUN), sums[:, :, halves[0]].rearrange(from_sums, i=RUN), ACT.Relu)
        nc.vector.tensor_scalar(
            woven[1][:, :VECTOR_PLACES, :].rearrange(to_woven, i=RUN), sums[:, :, HALF:cut].rearrange(from_sums, i=RUN), 0.0, None, ALU.max
        )
        nc.scalar.activation(woven[1][:, VECTOR_PLACES:, :].rearrange(to_woven, i=RUN), sums[:, :, cut:].rearrange(from_sums, i=RUN), ACT.Relu)

        out_rows = out.rearrange("(a p) o -> p a o", p=P)
        for h in range(2):
            hid_codes = sb.tile([P, HALF], U32, name="hid_codes%d" % h, align_bytes=64)
            hid_plane = sb.tile([P, HALF], U8, name="hid_plane%d" % h, align_bytes=64)
            nc.vector.quantize_mx(hid_codes[:].bitcast(E4M3X4), hid_plane[:], woven[h][:].rearrange("p o t -> p (o t)"))
            result = sb.tile([P, N // P, HALF], F32, name="result%d" % h)
            for a in range(N // P):
                acc = ps.tile([P, HALF], F32, name="second%d%d" % (h, a))
                cols = slice(a * P, (a + 1) * P)
                nc.tensor.matmul_mx(
                    out=acc[:],
                    lhsT=wb_codes[:, cols].bitcast(E4M3X4),
                    lhsT_scale=wb_plane[:, cols],
                    rhs=hid_codes[:].bitcast(E4M3X4),
                    rhs_scale=hid_plane[:],
                    start=True,
                    stop=True,
                )
                if a == 0:
                    nc.scalar.activation(result[:, a, :], acc[:], ACT.Copy)
                else:
                    nc.vector.tensor_copy(result[:, a, :], acc[:])
            nc.sync.dma_start(out_rows[:, :, halves[h]], result[:])
